import numpy as np
import ml_dtypes


def mxq(x, axis, fmt="e4m3"):
    dtype, down = {"e4m3": (ml_dtypes.float8_e4m3fn, 7), "e5m2": (ml_dtypes.float8_e5m2, 14)}[fmt]
    v = np.moveaxis(np.asarray(x, np.float32).astype(ml_dtypes.bfloat16).astype(np.float64), axis, -1)
    blocks = v.reshape(v.shape[:-1] + (-1, 32))
    amax = np.abs(blocks).max(-1, keepdims=True)
    byte = np.maximum(np.where(amax > 0, np.frexp(amax)[1] - 1 + 127, 0) - down, 1)
    scale = np.exp2(byte - 127.0)
    codes = (blocks / scale).astype(np.float32).astype(dtype).astype(np.float64)
    return np.moveaxis((codes * scale).reshape(v.shape), -1, axis)


WIDE = False


def mx_kscale(k):
    if not WIDE:
        return np.ones(k)
    levels = np.array([10, -10, 5, -5, 0])
    if k % 512:
        return np.exp2(np.random.permutation(np.resize(levels, k // 32))).repeat(32)
    a = np.empty((k // 512, 16))
    for p in range(k // 512):
        a[p, :8] = np.random.permutation(np.resize(levels, 8))
        for g in range(8):
            far = levels[np.abs(levels - a[p, g]) >= 10]
            a[p, g + 8] = far[np.random.randint(len(far))]
    return np.exp2(a.ravel()).repeat(32)


def f64(x):
    return np.asarray(x).astype(np.float64)


def striped(idx):
    return np.tile(idx.reshape(-1, 16).T, (8, 1)).astype(np.uint16)


def unstriped(offs):
    return offs[:16].T.reshape(-1).astype(np.int64)


def pack_weight(w):
    k, n = w.shape
    w = f64(np.asarray(w, np.float32).astype(ml_dtypes.bfloat16)).reshape(k // 32, 32, n)
    amax = np.abs(w).max(1)
    byte = np.clip(np.where(amax > 0, np.frexp(amax)[1] - 1 + 127 - 7, 1), 1, 254)
    scaled = (w * np.exp2(127.0 - byte)[:, None, :]).reshape(k, n).astype(np.float32)
    words = np.ascontiguousarray(scaled.reshape(k // 512, 128, 4, n).transpose(0, 1, 3, 2)).astype(ml_dtypes.float8_e4m3fn).view(np.uint8)
    return words, np.ascontiguousarray(byte.astype(np.uint8).reshape(k // 512, 16, n))


def unpack_weight(words, scales):
    g, p, n, _ = words.shape
    vals = np.ascontiguousarray(words).view(ml_dtypes.float8_e4m3fn).astype(np.float64) * np.repeat(np.exp2(scales.astype(np.float64) - 127.0), 8, axis=1)[..., None]
    return vals.transpose(0, 1, 3, 2).reshape(g * 512, n)


def gelu(v):
    return 0.5 * v * (1.0 + np.tanh(np.sqrt(2.0 / np.pi) * (v + 0.044715 * v**3)))


K, T, E, C, N = 1024, 1280, 6, 256, 256
TOP = 4
PAD = 64


def by_expert(wq, xq):
    return np.concatenate([wq[e].T @ xq[:, e * C:(e + 1) * C] for e in range(E)], axis=1)


def setup_inputs():
    n = np.random.standard_normal
    s = mx_kscale(K)[:, None]
    slot_token = np.empty(E * C, np.int64); pos = np.tile(E * C + np.arange(T) % PAD, (TOP, 1)); taken = np.zeros(T, np.int64)
    liked = np.random.randn(T)
    for e in np.random.permutation(E):
        free = np.flatnonzero(taken < TOP); pick = np.random.permutation(free[np.argsort(-(liked[free] + np.random.gumbel(size=free.size)))[:C]]); slot_token[e * C:(e + 1) * C] = pick
        pos[taken[pick], pick] = e * C + np.arange(C); taken[pick] += 1
    g = np.random.uniform(0.2, 0.8, (TOP, T))
    packed = [pack_weight(m) for m in n((E, K, N)) / np.sqrt(K) / s[None]]
    return {
        "xT": (n((K, T)) * s).astype(np.float32),
        "w_words": np.stack([m[0] for m in packed]),
        "w_scales": np.stack([m[1] for m in packed]),
        "b": (0.3 * n((N, E))).astype(np.float32),
        "gate": np.stack([np.tile(r, (N, 1)) for r in g]).astype(np.float32),
        "offs": striped(slot_token),
        "pos1": striped(pos[0]),
        "pos2": striped(pos[1]),
        "pos3": striped(pos[2]),
        "pos4": striped(pos[3]),
    }


def reference(xT, w_words, w_scales, b, gate, offs, pos1, pos2, pos3, pos4):
    idx = unstriped(offs)
    w = np.stack([unpack_weight(w_words[e], w_scales[e]) for e in range(E)])
    xq = mxq(f64(xT)[:, idx], 0, "e4m3")
    y = by_expert(w, xq)
    y = gelu(y + np.repeat(f64(b), C, axis=1))
    y = np.concatenate([y, np.zeros((N, PAD))], axis=1)
    return sum(f64(gate[r]) * y[:, unstriped(p)] for r, p in enumerate((pos1, pos2, pos3, pos4)))

@@ -1,0 +1,174 @@
+from contextlib import ExitStack
+
+import concourse.mybir as mybir
+from concourse.masks import make_identity
+
+K, T, E, C, N = 1024, 1280, 6, 256, 256
+TOP, PAD = 4, 64
+S = E * C
+FLOPS = 2 * K * N * S
+BYTES = 4 * K * T + E * K * N + E * (K // 32) * N + 4 * N * E + 4 * TOP * T + 2 * 128 * (S + TOP * T) // 16 + 4 * N * T
+
+F32 = mybir.dt.float32
+BF16 = mybir.dt.bfloat16
+I32 = mybir.dt.int32
+U32 = mybir.dt.uint32
+U16 = mybir.dt.uint16
+U8 = mybir.dt.uint8
+FP8X4 = mybir.dt.float8_e4m3fn_x4
+ACT = mybir.ActivationFunctionType
+ALU = mybir.AluOpType
+
+P = 128
+PASSES = 2
+HALVES = 2
+X_CHUNKS = [(0, 0, 512, 256), (0, 512, 512, 256), (0, 1024, 256, 128), (1, 0, 512, 0), (1, 512, 512, 320), (1, 1024, 256, 160)]
+WORD0_PIECES = [(0, 768), (768, 768)]
+BYTE_PIECES = [(0, 768), (768, 768)]
+WORD1_PIECES = [(0, 512), (512, 512), (1024, 256), (1280, 256)]
+W_PIECES = [(0, 2), (2, 2), (4, 2)]
+GATE_CHUNKS = [(0, 512), (512, 512), (1024, 256)]
+OUT_CHUNKS = [(0, 0, 512, False), (0, 512, 512, False), (0, 1024, 256, False), (1, 0, 512, False), (1, 512, 512, False), (1, 1024, 256, True)]
+
+
+def piece_of(pieces, tiles, first, width):
+    for (start, size), tile in zip(pieces, tiles):
+        if start <= first and first + width <= start + size:
+            return tile, first - start
+    raise ValueError("no piece")
+
+
+def tile_moe_ecr_lin_gelu_kernel(tc, xT, w_words, w_scales, b, gate, offs, pos1, pos2, pos3, pos4, out):
+    nc = tc.nc
+    with ExitStack() as ctx:
+        keep = ctx.enter_context(tc.tile_pool(name="keep", bufs=1))
+        ring = ctx.enter_context(tc.tile_pool(name="ring", bufs=2))
+        mm_psum = ctx.enter_context(tc.psum_pool(name="mm_psum", bufs=4))
+        sum_psum = ctx.enter_context(tc.psum_pool(name="sum_psum", bufs=2))
+
+        x_scales = keep.tile([P, T], U8, name="x_scales", align_bytes=64)
+        w_planes = keep.tile([P, E * PASSES * N], U8, name="w_planes", align_bytes=64)
+        zeros = keep.tile([P, PAD], F32, name="zeros")
+        nc.vector.memset(w_planes[:].bitcast(I32), 0)
+        nc.vector.memset(x_scales[:].bitcast(I32), 0)
+        nc.vector.memset(zeros[:], 0.0)
+        y = [keep.tile([P, S + PAD], F32, name="y%d" % h) for h in range(HALVES)]
+        for h in range(HALVES):
+            nc.scalar.activation(out=y[h][:, S:], in_=zeros[:], func=ACT.Gelu_apprx_tanh)
+        ident = keep.tile([P, P], F32, name="ident")
+        make_identity(nc, ident[:])
+
+        x_raw = []
+        slot_tokens = keep.tile([P, S // 16], U16, name="slot_tokens")
+        for i, (a, t0, w, unused) in enumerate(X_CHUNKS):
+            raw = keep.tile([P, 4, w], F32, name="x_raw%d" % i)
+            nc.sync.dma_start(out=raw[:], in_=xT[512 * a : 512 * (a + 1), t0 : t0 + w].rearrange("(p j) t -> p j t", j=4))
+            x_raw.append(raw)
+            if i == 1:
+                nc.sync.dma_start(slot_tokens[:], offs)
+        w_codes = []
+        for i, (e0, ne) in enumerate(W_PIECES):
+            wt = keep.tile([P, ne * PASSES * N], U32, name="w_codes%d" % i, align_bytes=64)
+            nc.sync.dma_start(
+                out=wt[:].bitcast(I32).rearrange("p (g n) -> p g n", n=N),
+                in_=w_words[e0 : e0 + ne].rearrange("e a p n r -> p (e a) (n r)").bitcast(I32),
+            )
+            w_codes.append(wt)
+            if i == 0:
+                for r in range(4):
+                    nc.sync.dma_start(
+                        out=w_planes[r:P:32, :].bitcast(I32).rearrange("q (g n) -> q g n", n=N // 4),
+                        in_=w_scales[:, :, r:16:4, :].rearrange("e a q n -> q (e a) n").bitcast(I32),
+                    )
+                bias = keep.tile([P, HALVES, 8], F32, name="bias")
+                nc.sync.dma_start(out=bias[:, :, 0:E], in_=b.rearrange("(h p) e -> p h e", p=P))
+        token_slots = []
+        for r, pos in enumerate((pos1, pos2, pos3, pos4)):
+            lst = keep.tile([P, T // 16], U16, name="token_slots%d" % r)
+            nc.sync.dma_start(lst[:], pos)
+            token_slots.append(lst)
+        gates = []
+        for i, (t0, w) in enumerate(GATE_CHUNKS):
+            g = keep.tile([P, TOP, w], F32, name="gates%d" % i)
+            nc.sync.dma_start(out=g[:], in_=gate[:, 0:P, t0 : t0 + w].rearrange("r p t -> p r t"))
+            gates.append(g)
+
+        x_codes = [keep.tile([P, T], U32, name="x_codes%d" % a, align_bytes=64) for a in range(PASSES)]
+        g_codes = [[], []]
+        g_scales = []
+
+        def gather(window, pieces, dtype, label, tiles):
+            for s0, w in pieces:
+                got = keep.tile([P, w], dtype, name="%s_%d" % (label, s0), align_bytes=64)
+                nc.vector.tensor_copy(got[:], window[:].indirect(slot_tokens[:, s0 // 16 : (s0 + w) // 16]))
+                tiles.append(got)
+
+        for i, (a, t0, w, wv) in enumerate(X_CHUNKS):
+            grouped = keep.tile([P, w, 4], BF16, name="grouped%d" % i, align_bytes=64)
+            if wv < w:
+                nc.scalar.activation(
+                    out=grouped[:, wv:, :].rearrange("p (c i) j -> p c j i", i=4),
+                    in_=x_raw[i][:, :, wv:].rearrange("p j (c i) -> p c j i", i=4),
+                    func=ACT.Copy,
+                )
+            if wv > 0:
+                nc.vector.tensor_copy(
+                    out=grouped[:, :wv, :].rearrange("p (c i) j -> p c j i", i=4),
+                    in_=x_raw[i][:, :, :wv].rearrange("p j (c i) -> p c j i", i=4),
+                )
+            nc.vector.quantize_mx(
+                out=x_codes[a][:, t0 : t0 + w].bitcast(FP8X4),
+                scales=x_scales[4 * a :, t0 : t0 + w],
+                in_=grouped[:].rearrange("p t j -> p (t j)"),
+            )
+            if a == 0 and t0 + w == T:
+                gather(x_codes[0], WORD0_PIECES, U32, "g0", g_codes[0])
+        gather(x_scales, BYTE_PIECES, U8, "gs", g_scales)
+        gather(x_codes[1], WORD1_PIECES, U32, "g1", g_codes[1])
+
+        for h in range(HALVES):
+            for e in range(E):
+                acc = mm_psum.tile([P, C], F32, name="acc")
+                wt, e_in = piece_of(W_PIECES, w_codes, e, 1)
+                gs, s_off = piece_of(BYTE_PIECES, g_scales, e * C, C)
+                for a in range(PASSES):
+                    gc, c_off = piece_of((WORD0_PIECES, WORD1_PIECES)[a], g_codes[a], e * C, C)
+                    wc = (e_in * PASSES + a) * N + h * P
+                    ws = (e * PASSES + a) * N + h * P
+                    nc.tensor.matmul_mx(
+                        out=acc[:],
+                        lhsT=wt[:, wc : wc + P].bitcast(FP8X4),
+                        lhsT_scale=w_planes[:, ws : ws + P],
+                        rhs=gc[:, c_off : c_off + C].bitcast(FP8X4),
+                        rhs_scale=gs[4 * a :, s_off : s_off + C],
+                        start=(a == 0),
+                        stop=(a == PASSES - 1),
+                    )
+                nc.scalar.activation(out=y[h][:, e * C : (e + 1) * C], in_=acc[:], func=ACT.Gelu_apprx_tanh, bias=bias[:, h, e : e + 1])
+
+        for h, t0, w, on_vector in OUT_CHUNKS:
+            g, g_off = piece_of(GATE_CHUNKS, gates, t0, w)
+            prods = []
+            for r in range(TOP):
+                prod = ring.tile([P, w], F32, name="prod%d" % r)
+                nc.vector.tensor_tensor(prod[:], y[h][:].indirect(token_slots[r][:, t0 // 16 : (t0 + w) // 16]), g[:, r, g_off : g_off + w], ALU.mult)
+                prods.append(prod)
+            result = ring.tile([P, w], F32, name="result")
+            if on_vector:
+                left = ring.tile([P, w], F32, name="left")
+                right = ring.tile([P, w], F32, name="right")
+                nc.vector.tensor_tensor(left[:], prods[0][:], prods[1][:], ALU.add)
+                nc.vector.tensor_tensor(right[:], prods[2][:], prods[3][:], ALU.add)
+                nc.vector.tensor_tensor(result[:], left[:], right[:], ALU.add)
+            else:
+                turned = sum_psum.tile([P, w], F32, name="turned")
+                for c0 in range(0, w, P):
+                    for r in range(TOP):
+                        nc.tensor.matmul(turned[:, c0 : c0 + P], lhsT=prods[r][:, c0 : c0 + P], rhs=ident[:], is_transpose=True, start=(r == 0), stop=(r == TOP - 1))
+                turned_sb = ring.tile([P, w], F32, name="turned_sb")
+                nc.scalar.copy(out=turned_sb[:], in_=turned[:])
+                back = sum_psum.tile([P, w], F32, name="back")
+                for c0 in range(0, w, P):
+                    nc.tensor.transpose(back[:, c0 : c0 + P], turned_sb[:, c0 : c0 + P], ident[:])
+                nc.scalar.copy(out=result[:], in_=back[:])
+            nc.sync.dma_start(out=out[h * P : (h + 1) * P, t0 : t0 + w], in_=result[:])

@@ -22,13 +22,15 @@ ALU = mybir.AluOpType
 P = 128
 PASSES = 2
 HALVES = 2
-X_CHUNKS = [(0, 0, 512, 256), (0, 512, 512, 256), (0, 1024, 256, 128), (1, 0, 512, 0), (1, 512, 512, 320), (1, 1024, 256, 160)]
+X_CHUNKS = [(0, 0, 512, 384), (0, 512, 256, 192), (0, 768, 256, 192), (0, 1024, 256, 192), (1, 0, 256, 0), (1, 256, 256, 0), (1, 512, 256, 0), (1, 768, 256, 128), (1, 1024, 256, 192)]
 WORD0_PIECES = [(0, 768), (768, 768)]
 BYTE_PIECES = [(0, 768), (768, 768)]
-WORD1_PIECES = [(0, 512), (512, 512), (1024, 256), (1280, 256)]
+WORD1_PIECES = [(0, 768), (768, 256), (1024, 256), (1280, 256)]
 W_PIECES = [(0, 2), (2, 2), (4, 2)]
-GATE_CHUNKS = [(0, 512), (512, 512), (1024, 256)]
-OUT_CHUNKS = [(0, 0, 512, False), (0, 512, 512, False), (0, 1024, 256, False), (1, 0, 512, False), (1, 512, 512, False), (1, 1024, 256, True)]
+GATE_CHUNKS = [(0, 256), (256, 512), (768, 512)]
+PART = 256
+PE_CHUNKS = [(0, 0, 256), (0, 256, 512), (0, 768, 512), (1, 768, 512), (1, 256, 256), (1, 512, 128)]
+VECTOR_CHUNKS = [(1, 0, 256), (1, 640, 128)]
 
 
 def piece_of(pieces, tiles, first, width):
@@ -42,9 +44,9 @@ def tile_moe_ecr_lin_gelu_kernel(tc, xT, w_words, w_scales, b, gate, offs, pos1,
     nc = tc.nc
     with ExitStack() as ctx:
         keep = ctx.enter_context(tc.tile_pool(name="keep", bufs=1))
-        ring = ctx.enter_context(tc.tile_pool(name="ring", bufs=2))
+        ring = ctx.enter_context(tc.tile_pool(name="ring", bufs=3))
         mm_psum = ctx.enter_context(tc.psum_pool(name="mm_psum", bufs=4))
-        sum_psum = ctx.enter_context(tc.psum_pool(name="sum_psum", bufs=2))
+        sum_psum = ctx.enter_context(tc.psum_pool(name="sum_psum", bufs=4))
 
         x_scales = keep.tile([P, T], U8, name="x_scales", align_bytes=64)
         w_planes = keep.tile([P, E * PASSES * N], U8, name="w_planes", align_bytes=64)
@@ -123,8 +125,10 @@ def tile_moe_ecr_lin_gelu_kernel(tc, xT, w_words, w_scales, b, gate, offs, pos1,
             )
             if a == 0 and t0 + w == T:
                 gather(x_codes[0], WORD0_PIECES, U32, "g0", g_codes[0])
-        gather(x_scales, BYTE_PIECES, U8, "gs", g_scales)
-        gather(x_codes[1], WORD1_PIECES, U32, "g1", g_codes[1])
+        gather(x_scales, BYTE_PIECES[:1], U8, "gs", g_scales)
+        gather(x_codes[1], WORD1_PIECES[:1], U32, "g1", g_codes[1])
+        gather(x_scales, BYTE_PIECES[1:], U8, "gs", g_scales)
+        gather(x_codes[1], WORD1_PIECES[1:], U32, "g1", g_codes[1])
 
         for h in range(HALVES):
             for e in range(E):
@@ -146,29 +150,52 @@ def tile_moe_ecr_lin_gelu_kernel(tc, xT, w_words, w_scales, b, gate, offs, pos1,
                     )
                 nc.scalar.activation(out=y[h][:, e * C : (e + 1) * C], in_=acc[:], func=ACT.Gelu_apprx_tanh, bias=bias[:, h, e : e + 1])
 
-        for h, t0, w, on_vector in OUT_CHUNKS:
+        def products(h, t0, w):
             g, g_off = piece_of(GATE_CHUNKS, gates, t0, w)
             prods = []
             for r in range(TOP):
                 prod = ring.tile([P, w], F32, name="prod%d" % r)
                 nc.vector.tensor_tensor(prod[:], y[h][:].indirect(token_slots[r][:, t0 // 16 : (t0 + w) // 16]), g[:, r, g_off : g_off + w], ALU.mult)
                 prods.append(prod)
+            return prods
+
+        waiting = []
+        for step in PE_CHUNKS + [(0, 0, 0)]:
+            h, t0, w = step
+            parts = [(c0, min(PART, w - c0)) for c0 in range(0, w, PART)]
+            count = max(len(parts), len(waiting))
+            widths = [(parts[i][1] if i < len(parts) else 0, waiting[i][2] if i < len(waiting) else 0) for i in range(count)]
+            banks = [sum_psum.tile([P, a + c], F32, name="bank") for a, c in widths]
+            if w:
+                prods = products(*step)
+                for r in range(TOP):
+                    for c0 in range(0, w, P):
+                        col = c0 % PART
+                        last = min(PART, w - c0 + col) - P
+                        nc.tensor.matmul(
+                            banks[c0 // PART][:, col : col + P], lhsT=prods[r][:, c0 : c0 + P], rhs=ident[:], is_transpose=True,
+                            start=(r == 0 and col == 0), stop=(r == TOP - 1 and col == last),
+                        )
+            for i, (hb, tb, wb, sums) in enumerate(waiting):
+                for c0 in range(0, wb, P):
+                    at = widths[i][0] + c0
+                    nc.tensor.transpose(banks[i][:, at : at + P], sums[:, c0 : c0 + P], ident[:])
+            now = []
+            for i in range(count):
+                staged = ring.tile([P, sum(widths[i])], F32, name="staged", bufs=6)
+                nc.scalar.copy(out=staged[:], in_=banks[i][:])
+                if i < len(waiting):
+                    hb, tb, wb, sums = waiting[i]
+                    nc.sync.dma_start(out=out[hb * P : (hb + 1) * P, tb : tb + wb], in_=staged[:, widths[i][0] :])
+                if i < len(parts):
+                    now.append((h, t0 + parts[i][0], parts[i][1], staged))
+            waiting = now
+        for h, t0, w in VECTOR_CHUNKS:
+            prods = products(h, t0, w)
+            left = ring.tile([P, w], F32, name="left")
+            right = ring.tile([P, w], F32, name="right")
             result = ring.tile([P, w], F32, name="result")
-            if on_vector:
-                left = ring.tile([P, w], F32, name="left")
-                right = ring.tile([P, w], F32, name="right")
-                nc.vector.tensor_tensor(left[:], prods[0][:], prods[1][:], ALU.add)
-                nc.vector.tensor_tensor(right[:], prods[2][:], prods[3][:], ALU.add)
-                nc.vector.tensor_tensor(result[:], left[:], right[:], ALU.add)
-            else:
-                turned = sum_psum.tile([P, w], F32, name="turned")
-                for c0 in range(0, w, P):
-                    for r in range(TOP):
-                        nc.tensor.matmul(turned[:, c0 : c0 + P], lhsT=prods[r][:, c0 : c0 + P], rhs=ident[:], is_transpose=True, start=(r == 0), stop=(r == TOP - 1))
-                turned_sb = ring.tile([P, w], F32, name="turned_sb")
-                nc.scalar.copy(out=turned_sb[:], in_=turned[:])
-                back = sum_psum.tile([P, w], F32, name="back")
-                for c0 in range(0, w, P):
-                    nc.tensor.transpose(back[:, c0 : c0 + P], turned_sb[:, c0 : c0 + P], ident[:])
-                nc.scalar.copy(out=result[:], in_=back[:])
+            nc.vector.tensor_tensor(left[:], prods[0][:], prods[1][:], ALU.add)
+            nc.vector.tensor_tensor(right[:], left[:], prods[2][:], ALU.add)
+            nc.vector.tensor_tensor(result[:], right[:], prods[3][:], ALU.add)
             nc.sync.dma_start(out=out[h * P : (h + 1) * P, t0 : t0 + w], in_=result[:])

from contextlib import ExitStack

import concourse.mybir as mybir
from concourse.masks import make_identity

K, T, E, C, N = 1024, 1280, 6, 256, 256
TOP, PAD = 4, 64
S = E * C
FLOPS = 2 * K * N * S
BYTES = 4 * K * T + E * K * N + E * (K // 32) * N + 4 * N * E + 4 * TOP * T + 2 * 128 * (S + TOP * T) // 16 + 4 * N * T

F32 = mybir.dt.float32
BF16 = mybir.dt.bfloat16
I32 = mybir.dt.int32
U32 = mybir.dt.uint32
U16 = mybir.dt.uint16
U8 = mybir.dt.uint8
FP8X4 = mybir.dt.float8_e4m3fn_x4
ACT = mybir.ActivationFunctionType
ALU = mybir.AluOpType

P = 128
PASSES = 2
HALVES = 2
X_CHUNKS = [(0, 0, 512, 384), (0, 512, 256, 192), (0, 768, 256, 192), (0, 1024, 256, 192), (1, 0, 256, 0), (1, 256, 256, 0), (1, 512, 256, 0), (1, 768, 256, 128), (1, 1024, 256, 192)]
WORD0_PIECES = [(0, 768), (768, 768)]
BYTE_PIECES = [(0, 768), (768, 768)]
WORD1_PIECES = [(0, 768), (768, 256), (1024, 256), (1280, 256)]
W_PIECES = [(0, 2), (2, 2), (4, 2)]
GATE_CHUNKS = [(0, 256), (256, 512), (768, 512)]
PART = 256
PE_CHUNKS = [(0, 0, 256), (0, 256, 512), (0, 768, 512), (1, 768, 512), (1, 256, 256), (1, 512, 128)]
VECTOR_CHUNKS = [(1, 0, 256), (1, 640, 128)]


def piece_of(pieces, tiles, first, width):
    for (start, size), tile in zip(pieces, tiles):
        if start <= first and first + width <= start + size:
            return tile, first - start
    raise ValueError("no piece")


def tile_moe_ecr_lin_gelu_kernel(tc, xT, w_words, w_scales, b, gate, offs, pos1, pos2, pos3, pos4, out):
    nc = tc.nc
    with ExitStack() as ctx:
        keep = ctx.enter_context(tc.tile_pool(name="keep", bufs=1))
        ring = ctx.enter_context(tc.tile_pool(name="ring", bufs=3))
        mm_psum = ctx.enter_context(tc.psum_pool(name="mm_psum", bufs=4))
        sum_psum = ctx.enter_context(tc.psum_pool(name="sum_psum", bufs=4))

        x_scales = keep.tile([P, T], U8, name="x_scales", align_bytes=64)
        w_planes = keep.tile([P, E * PASSES * N], U8, name="w_planes", align_bytes=64)
        zeros = keep.tile([P, PAD], F32, name="zeros")
        nc.vector.memset(w_planes[:].bitcast(I32), 0)
        nc.vector.memset(x_scales[:].bitcast(I32), 0)
        nc.vector.memset(zeros[:], 0.0)
        y = [keep.tile([P, S + PAD], F32, name="y%d" % h) for h in range(HALVES)]
        for h in range(HALVES):
            nc.scalar.activation(out=y[h][:, S:], in_=zeros[:], func=ACT.Gelu_apprx_tanh)
        ident = keep.tile([P, P], F32, name="ident")
        make_identity(nc, ident[:])

        x_raw = []
        slot_tokens = keep.tile([P, S // 16], U16, name="slot_tokens")
        for i, (a, t0, w, unused) in enumerate(X_CHUNKS):
            raw = keep.tile([P, 4, w], F32, name="x_raw%d" % i)
            nc.sync.dma_start(out=raw[:], in_=xT[512 * a : 512 * (a + 1), t0 : t0 + w].rearrange("(p j) t -> p j t", j=4))
            x_raw.append(raw)
            if i == 1:
                nc.sync.dma_start(slot_tokens[:], offs)
        w_codes = []
        for i, (e0, ne) in enumerate(W_PIECES):
            wt = keep.tile([P, ne * PASSES * N], U32, name="w_codes%d" % i, align_bytes=64)
            nc.sync.dma_start(
                out=wt[:].bitcast(I32).rearrange("p (g n) -> p g n", n=N),
                in_=w_words[e0 : e0 + ne].rearrange("e a p n r -> p (e a) (n r)").bitcast(I32),
            )
            w_codes.append(wt)
            if i == 0:
                for r in range(4):
                    nc.sync.dma_start(
                        out=w_planes[r:P:32, :].bitcast(I32).rearrange("q (g n) -> q g n", n=N // 4),
                        in_=w_scales[:, :, r:16:4, :].rearrange("e a q n -> q (e a) n").bitcast(I32),
                    )
                bias = keep.tile([P, HALVES, 8], F32, name="bias")
                nc.sync.dma_start(out=bias[:, :, 0:E], in_=b.rearrange("(h p) e -> p h e", p=P))
        token_slots = []
        for r, pos in enumerate((pos1, pos2, pos3, pos4)):
            lst = keep.tile([P, T // 16], U16, name="token_slots%d" % r)
            nc.sync.dma_start(lst[:], pos)
            token_slots.append(lst)
        gates = []
        for i, (t0, w) in enumerate(GATE_CHUNKS):
            g = keep.tile([P, TOP, w], F32, name="gates%d" % i)
            nc.sync.dma_start(out=g[:], in_=gate[:, 0:P, t0 : t0 + w].rearrange("r p t -> p r t"))
            gates.append(g)

        x_codes = [keep.tile([P, T], U32, name="x_codes%d" % a, align_bytes=64) for a in range(PASSES)]
        g_codes = [[], []]
        g_scales = []

        def gather(window, pieces, dtype, label, tiles):
            for s0, w in pieces:
                got = keep.tile([P, w], dtype, name="%s_%d" % (label, s0), align_bytes=64)
                nc.vector.tensor_copy(got[:], window[:].indirect(slot_tokens[:, s0 // 16 : (s0 + w) // 16]))
                tiles.append(got)

        for i, (a, t0, w, wv) in enumerate(X_CHUNKS):
            grouped = keep.tile([P, w, 4], BF16, name="grouped%d" % i, align_bytes=64)
            if wv < w:
                nc.scalar.activation(
                    out=grouped[:, wv:, :].rearrange("p (c i) j -> p c j i", i=4),
                    in_=x_raw[i][:, :, wv:].rearrange("p j (c i) -> p c j i", i=4),
                    func=ACT.Copy,
                )
            if wv > 0:
                nc.vector.tensor_copy(
                    out=grouped[:, :wv, :].rearrange("p (c i) j -> p c j i", i=4),
                    in_=x_raw[i][:, :, :wv].rearrange("p j (c i) -> p c j i", i=4),
                )
            nc.vector.quantize_mx(
                out=x_codes[a][:, t0 : t0 + w].bitcast(FP8X4),
                scales=x_scales[4 * a :, t0 : t0 + w],
                in_=grouped[:].rearrange("p t j -> p (t j)"),
            )
            if a == 0 and t0 + w == T:
                gather(x_codes[0], WORD0_PIECES, U32, "g0", g_codes[0])
        gather(x_scales, BYTE_PIECES[:1], U8, "gs", g_scales)
        gather(x_codes[1], WORD1_PIECES[:1], U32, "g1", g_codes[1])
        gather(x_scales, BYTE_PIECES[1:], U8, "gs", g_scales)
        gather(x_codes[1], WORD1_PIECES[1:], U32, "g1", g_codes[1])

        for h in range(HALVES):
            for e in range(E):
                acc = mm_psum.tile([P, C], F32, name="acc")
                wt, e_in = piece_of(W_PIECES, w_codes, e, 1)
                gs, s_off = piece_of(BYTE_PIECES, g_scales, e * C, C)
                for a in range(PASSES):
                    gc, c_off = piece_of((WORD0_PIECES, WORD1_PIECES)[a], g_codes[a], e * C, C)
                    wc = (e_in * PASSES + a) * N + h * P
                    ws = (e * PASSES + a) * N + h * P
                    nc.tensor.matmul_mx(
                        out=acc[:],
                        lhsT=wt[:, wc : wc + P].bitcast(FP8X4),
                        lhsT_scale=w_planes[:, ws : ws + P],
                        rhs=gc[:, c_off : c_off + C].bitcast(FP8X4),
                        rhs_scale=gs[4 * a :, s_off : s_off + C],
                        start=(a == 0),
                        stop=(a == PASSES - 1),
                    )
                nc.scalar.activation(out=y[h][:, e * C : (e + 1) * C], in_=acc[:], func=ACT.Gelu_apprx_tanh, bias=bias[:, h, e : e + 1])

        def products(h, t0, w):
            g, g_off = piece_of(GATE_CHUNKS, gates, t0, w)
            prods = []
            for r in range(TOP):
                prod = ring.tile([P, w], F32, name="prod%d" % r)
                nc.vector.tensor_tensor(prod[:], y[h][:].indirect(token_slots[r][:, t0 // 16 : (t0 + w) // 16]), g[:, r, g_off : g_off + w], ALU.mult)
                prods.append(prod)
            return prods

        waiting = []
        for step in PE_CHUNKS + [(0, 0, 0)]:
            h, t0, w = step
            parts = [(c0, min(PART, w - c0)) for c0 in range(0, w, PART)]
            count = max(len(parts), len(waiting))
            widths = [(parts[i][1] if i < len(parts) else 0, waiting[i][2] if i < len(waiting) else 0) for i in range(count)]
            banks = [sum_psum.tile([P, a + c], F32, name="bank") for a, c in widths]
            if w:
                prods = products(*step)
                for r in range(TOP):
                    for c0 in range(0, w, P):
                        col = c0 % PART
                        last = min(PART, w - c0 + col) - P
                        nc.tensor.matmul(
                            banks[c0 // PART][:, col : col + P], lhsT=prods[r][:, c0 : c0 + P], rhs=ident[:], is_transpose=True,
                            start=(r == 0 and col == 0), stop=(r == TOP - 1 and col == last),
                        )
            for i, (hb, tb, wb, sums) in enumerate(waiting):
                for c0 in range(0, wb, P):
                    at = widths[i][0] + c0
                    nc.tensor.transpose(banks[i][:, at : at + P], sums[:, c0 : c0 + P], ident[:])
            now = []
            for i in range(count):
                staged = ring.tile([P, sum(widths[i])], F32, name="staged", bufs=6)
                nc.scalar.copy(out=staged[:], in_=banks[i][:])
                if i < len(waiting):
                    hb, tb, wb, sums = waiting[i]
                    nc.sync.dma_start(out=out[hb * P : (hb + 1) * P, tb : tb + wb], in_=staged[:, widths[i][0] :])
                if i < len(parts):
                    now.append((h, t0 + parts[i][0], parts[i][1], staged))
            waiting = now
        for h, t0, w in VECTOR_CHUNKS:
            prods = products(h, t0, w)
            left = ring.tile([P, w], F32, name="left")
            right = ring.tile([P, w], F32, name="right")
            result = ring.tile([P, w], F32, name="result")
            nc.vector.tensor_tensor(left[:], prods[0][:], prods[1][:], ALU.add)
            nc.vector.tensor_tensor(right[:], left[:], prods[2][:], ALU.add)
            nc.vector.tensor_tensor(result[:], right[:], prods[3][:], ALU.add)
            nc.sync.dma_start(out=out[h * P : (h + 1) * P, t0 : t0 + w], in_=result[:])
